import numpy as np, ml_dtypes
CORES = [23,119,17,113]
N = 4
import mx_ref
NC, G = 128, 4
C = np.float32(0.019)
BF = ml_dtypes.bfloat16
def cut(t, i, w=512):
    return t[:, w * i:w * i + w]
def tile(rs):
    return np.stack(rs, axis=2).reshape(128, -1).astype(BF)
def layer(w, X):
    out = []
    for i in range(G):
        for t in range(len(X)):
            p = mx_ref.matmul(mx_ref.quantize(cut(w, len(X) * i + t)), X[t])
            z = p if t == 0 else z + p
        out.append(z)
    return out
def act(Z):
    return [np.maximum(z, 0) * C for z in Z]
def setup_inputs(rng):
    def f(*shape):
        return mx_ref.flush((rng.standard_normal(shape, dtype=np.float32) * np.exp2(rng.integers(-2, 3, shape[:-1] + (1,)))).astype(BF))
    return {"xk": f(N, 128, 512), "xq": f(N, 128, 4 * NC), "wk": f(N, 128, G * 512), "wq": f(N, 128, G * 512)}
def setup_inputs_blocks(rng):
    d = setup_inputs(rng)
    for k in ("xk", "xq", "wk", "wq"): d[k] = mx_ref.spread(d[k], rng, 4)
    return d
def setup_inputs_wide(rng):
    d = setup_inputs(rng)
    for k in ("xk", "xq", "wk", "wq"): d[k] = mx_ref.flush((d[k].astype(np.float32) * np.exp2(rng.integers(-5, 6, (N, 1, 1))).astype(np.float32)).astype(BF))
    return d
def reference(xk, xq, wk, wq):
    K = [mx_ref.quantize(tile(act(layer(wk[j], [mx_ref.quantize(xk[j])])))) for j in range(N)]
    y = np.zeros((N, 128, N * NC), np.float32)
    for r in range(N):
        q = mx_ref.quantize(tile(act(layer(wq[r], [mx_ref.quantize(xq[r])]))))
        for j in range(N):
            y[r][:, NC * j:NC * j + NC] = mx_ref.matmul(K[j], q)
    return {"y": y}

@@ -1,0 +1,157 @@
+from concourse.bass import DstId, RemoteDMATransfer
+from concourse.mybir import dt, ActivationFunctionType
+
+N, NC, G = 4, 128, 4
+TW = 4 * NC
+BANK = 512
+C = 0.019
+
+SCRATCH = {
+    "xk_t": ("sbuf", [128, TW], "bfloat16"), "wk_t": ("sbuf", [128, G * TW], "bfloat16"),
+    "xq_t": ("sbuf", [128, TW], "bfloat16"), "wq_t": ("sbuf", [128, G * TW], "bfloat16"),
+    "xk_c": ("sbuf", [128, NC], "float8_e4m3fn_x4"), "xk_s": ("sbuf", [128, NC], "uint8"),
+    "wk_c": ("sbuf", [128, G * NC], "float8_e4m3fn_x4"), "wk_s": ("sbuf", [128, G * NC], "uint8"),
+    "xq_c": ("sbuf", [128, NC], "float8_e4m3fn_x4"), "xq_s": ("sbuf", [128, NC], "uint8"),
+    "wq_c": ("sbuf", [128, G * NC], "float8_e4m3fn_x4"), "wq_s": ("sbuf", [128, G * NC], "uint8"),
+    "k_t": ("sbuf", [128, TW], "bfloat16"), "q_t": ("sbuf", [128, TW], "bfloat16"),
+    "q_c": ("sbuf", [128, NC], "float8_e4m3fn_x4"), "q_s": ("sbuf", [128, NC], "uint8"),
+    "ka_c": ("sbuf", [128, N * NC], "float8_e4m3fn_x4"), "ka_s": ("sbuf", [128, N * NC], "uint8"),
+    "zk": ("psum", [128, G * BANK], "float32"), "zq": ("psum", [128, G * BANK], "float32"),
+    "y_t": ("sbuf", [128, N * NC], "float32"),
+}
+SEMAPHORES = (["ld_xk", "ld_wk", "ld_xq", "ld_wq", "q_xk", "q_xq", "a_k", "a_q", "kq", "qq",
+               "sent_far", "sent_near", "st_a", "st_b"]
+              + ["q_wk%d" % i for i in range(G)] + ["q_wq%d" % i for i in range(G)]
+              + ["z_k%d" % i for i in range(G)] + ["z_q%d" % i for i in range(G)]
+              + ["arr%d" % j for j in range(N)] + ["y%d" % j for j in range(N)] + ["c%d" % j for j in range(N)])
+
+
+def _bits(mask):
+    return [1 << b for b in range(mask.bit_length()) if (mask >> b) & 1]
+
+
+def _join(bits):
+    m = 0
+    for b in bits:
+        m |= b
+    return m
+
+
+def _share(bits, parts):
+    n = 1
+    while 2 * n * parts <= len(bits):
+        n *= 2
+    return [_join(bits[p * n:(p + 1) * n]) for p in range(parts)]
+
+
+def _lanes(topo, cores, src):
+    far = [c for c in cores if c != src and topo.chip(c) != topo.chip(src)]
+    near = [c for c in cores if c != src and topo.chip(c) == topo.chip(src)]
+    out = 0
+    for c in far:
+        out |= topo.mask(src, c)
+    for c in far:
+        out &= topo.mask(src, c)
+    stay = 0
+    for c in near:
+        stay |= topo.mask(src, c)
+    if stay & ~out:
+        stay &= ~out
+    return (list(zip(far, _share(_bits(out), len(far)))) if far else [],
+            list(zip(near, _share(_bits(stay), len(near)))) if near else [])
+
+
+def _project(g, T, S, x, w, z, tile, tag):
+    g.tensor.wait_ge(S["q_x" + tag], 1)
+    for i in range(G):
+        g.tensor.wait_ge(S["q_w%s%d" % (tag, i)], 1)
+        g.tensor.matmul_mx(z[:, BANK * i:BANK * i + NC], w[0][:, NC * i:NC * i + NC], w[1][:, NC * i:NC * i + NC],
+                           x[0][:], x[1][:], True, True).then_inc(S["z_%s%d" % (tag, i)], 1)
+        g.scalar.wait_ge(S["z_%s%d" % (tag, i)], 1)
+        g.scalar.activation(tile[:, i:TW:4], z[:, BANK * i:BANK * i + NC], ActivationFunctionType.Relu,
+                            scale=C).then_inc(S["a_" + tag], 1)
+
+
+def _pack_inputs(g, T, S, xt, wt, x, w, tag):
+    g.vector.wait_ge(S["ld_x" + tag], 16)
+    g.vector.quantize_mx(x[0][:], x[1][:], xt[:]).then_inc(S["q_x" + tag], 1)
+    g.vector.wait_ge(S["ld_w" + tag], 16)
+    for i in range(G):
+        g.vector.quantize_mx(w[0][:, NC * i:NC * i + NC], w[1][:, NC * i:NC * i + NC],
+                             wt[:, TW * i:TW * i + TW]).then_inc(S["q_w%s%d" % (tag, i)], 1)
+
+
+def rank_program(g, core, T, topo):
+    r = T.rank_of(core)
+    if r is None:
+        return
+    S = T.sem
+    cores = list(T.cores)
+    far, near = _lanes(topo, cores, core)
+    for c, _m in far + near:
+        if not topo.may_write(core, c):
+            raise ValueError("no direct write from core %d to core %d" % (core, c))
+
+    def slot(j):
+        return slice(NC * j, NC * j + NC)
+
+    g.sync.dma_start(T.xk_t[:], T.xk[:]).then_inc(S.ld_xk, 16)
+    g.scalar.dma_start(T.wk_t[:], T.wk[:]).then_inc(S.ld_wk, 16)
+    g.sync.dma_start(T.xq_t[:], T.xq[:]).then_inc(S.ld_xq, 16)
+    g.scalar.dma_start(T.wq_t[:], T.wq[:]).then_inc(S.ld_wq, 16)
+
+    _pack_inputs(g, T, S, T.xk_t, T.wk_t, (T.xk_c, T.xk_s), (T.wk_c, T.wk_s), "k")
+    _project(g, T, S, (T.xk_c, T.xk_s), (T.wk_c, T.wk_s), T.zk, T.k_t, "k")
+    g.vector.wait_ge(S.a_k, G)
+    g.vector.quantize_mx(T.ka_c[:, slot(r)], T.ka_s[:, slot(r)], T.k_t[:]).then_inc(S.kq, 1)
+
+    codes = T.ka_c[:, slot(r)].bitcast(dt.uint8)
+    plane = T.ka_s[:, slot(r)]
+    g.wait_ge(S.kq, 1)
+    for ap in (codes, plane):
+        g.remote_dma_fused([RemoteDMATransfer(dst_ids=[DstId(rid=topo.addr(c)[0], pnc=topo.addr(c)[1])],
+                                              dma_engine_mask=m, remote_sem=S["arr%d" % r], src=ap, dst=ap)
+                            for c, m in far], local_sem=S.sent_far)
+    for ap in (codes, plane):
+        g.remote_dma_fused([RemoteDMATransfer(dst_ids=[DstId(rid=topo.addr(c)[0], pnc=topo.addr(c)[1])],
+                                              dma_engine_mask=m, remote_sem=S["arr%d" % r], src=ap, dst=ap)
+                            for c, m in near], local_sem=S.sent_near)
+
+    _pack_inputs(g, T, S, T.xq_t, T.wq_t, (T.xq_c, T.xq_s), (T.wq_c, T.wq_s), "q")
+    _project(g, T, S, (T.xq_c, T.xq_s), (T.wq_c, T.wq_s), T.zq, T.q_t, "q")
+    g.vector.wait_ge(S.a_q, G)
+    g.vector.quantize_mx(T.q_c[:], T.q_s[:], T.q_t[:]).then_inc(S.qq, 1)
+
+    def landed(j):
+        f, n = _lanes(topo, cores, cores[j])
+        return 2 * len(_bits(dict(f + n)[core]))
+
+    order = ([r] + [cores.index(c) for c, _m in near]
+             + sorted([cores.index(c) for c, _m in far], key=lambda j: topo.die(cores[j]) != topo.die(core)))
+    g.tensor.wait_ge(S.qq, 1)
+    g.tensor.wait_ge(S.kq, 1)
+    g.tensor.wait_ge(S.a_k, G)
+    g.sync.wait_ge(S.sent_far, 2 * sum(len(_bits(m)) for _c, m in far))
+    n_a = 0
+    for n, j in enumerate(order):
+        if j != r:
+            g.tensor.wait_ge(S["arr%d" % j], landed(j))
+        bank = T.zk[:, BANK * j:BANK * j + NC]
+        g.tensor.matmul_mx(bank, T.ka_c[:, slot(j)], T.ka_s[:, slot(j)], T.q_c[:], T.q_s[:],
+                           True, True).then_inc(S["y%d" % j], 1)
+        if n % 2 == 0:
+            g.vector.wait_ge(S["y%d" % j], 1)
+            g.vector.tensor_copy(T.y_t[:, slot(j)], bank).then_inc(S["c%d" % j], 1)
+        else:
+            g.scalar.wait_ge(S["y%d" % j], 1)
+            g.scalar.activation(T.y_t[:, slot(j)], bank, ActivationFunctionType.Copy).then_inc(S["c%d" % j], 1)
+        if n == len(order) - 1:
+            g.scalar.wait_ge(S["c%d" % j], 1)
+            g.scalar.dma_start(T.y[:, slot(j)], T.y_t[:, slot(j)]).then_inc(S.st_b, 16)
+        else:
+            g.sync.wait_ge(S["c%d" % j], 1)
+            g.sync.dma_start(T.y[:, slot(j)], T.y_t[:, slot(j)]).then_inc(S.st_a, 16)
+            n_a += 16
+    g.wait_ge(S.sent_near, 2 * sum(len(_bits(m)) for _c, m in near))
+    g.sync.wait_ge(S.st_a, n_a)
+    g.scalar.wait_ge(S.st_b, 16)

@@ -1,10 +1,12 @@
 from concourse.bass import DstId, RemoteDMATransfer
-from concourse.mybir import dt, ActivationFunctionType
+from concourse.mybir import dt, ActivationFunctionType, AluOpType
 
 N, NC, G = 4, 128, 4
 TW = 4 * NC
 BANK = 512
 C = 0.019
+WK_PIECES = ((0, 2), (2, 3), (3, 4))
+WQ_PIECES = ((0, 2), (2, 4))
 
 SCRATCH = {
     "xk_t": ("sbuf", [128, TW], "bfloat16"), "wk_t": ("sbuf", [128, G * TW], "bfloat16"),
@@ -19,66 +21,55 @@ SCRATCH = {
     "zk": ("psum", [128, G * BANK], "float32"), "zq": ("psum", [128, G * BANK], "float32"),
     "y_t": ("sbuf", [128, N * NC], "float32"),
 }
-SEMAPHORES = (["ld_xk", "ld_wk", "ld_xq", "ld_wq", "q_xk", "q_xq", "a_k", "a_q", "kq", "qq",
-               "sent_far", "sent_near", "st_a", "st_b"]
+SEMAPHORES = (["ld_xk", "ld_xq", "q_xk", "q_xq", "a_k", "a_q", "v_k", "v_q", "kq", "qq", "sent", "sent_p",
+               "st_a", "st_b"]
+              + ["ld_wk%d" % i for i in range(len(WK_PIECES))] + ["ld_wq%d" % i for i in range(len(WQ_PIECES))]
               + ["q_wk%d" % i for i in range(G)] + ["q_wq%d" % i for i in range(G)]
               + ["z_k%d" % i for i in range(G)] + ["z_q%d" % i for i in range(G)]
-              + ["arr%d" % j for j in range(N)] + ["y%d" % j for j in range(N)] + ["c%d" % j for j in range(N)])
+              + ["cd%d" % j for j in range(N)] + ["pl%d" % j for j in range(N)]
+              + ["y%d" % j for j in range(N)] + ["c%d" % j for j in range(N)])
 
 
-def _bits(mask):
-    return [1 << b for b in range(mask.bit_length()) if (mask >> b) & 1]
+def _count(mask):
+    return sum((mask >> b) & 1 for b in range(mask.bit_length()))
 
 
-def _join(bits):
-    m = 0
-    for b in bits:
-        m |= b
-    return m
+def _kin(topo, cores, me):
+    near = [c for c in cores if c != me and topo.chip(c) == topo.chip(me)]
+    far = [c for c in cores if topo.chip(c) != topo.chip(me)]
+    twin = [c for c in far if topo.die(c) == topo.die(me)]
+    cross = [c for c in far if topo.die(c) != topo.die(me)]
+    if len(near) != 1 or len(twin) != 1 or len(cross) != 1:
+        raise ValueError("the plan wants two ranks a chip, one a die")
+    return near[0], twin[0], cross[0]
 
 
-def _share(bits, parts):
-    n = 1
-    while 2 * n * parts <= len(bits):
-        n *= 2
-    return [_join(bits[p * n:(p + 1) * n]) for p in range(parts)]
-
-
-def _lanes(topo, cores, src):
-    far = [c for c in cores if c != src and topo.chip(c) != topo.chip(src)]
-    near = [c for c in cores if c != src and topo.chip(c) == topo.chip(src)]
-    out = 0
-    for c in far:
-        out |= topo.mask(src, c)
-    for c in far:
-        out &= topo.mask(src, c)
-    stay = 0
-    for c in near:
-        stay |= topo.mask(src, c)
-    if stay & ~out:
-        stay &= ~out
-    return (list(zip(far, _share(_bits(out), len(far)))) if far else [],
-            list(zip(near, _share(_bits(stay), len(near)))) if near else [])
-
-
-def _project(g, T, S, x, w, z, tile, tag):
-    g.tensor.wait_ge(S["q_x" + tag], 1)
-    for i in range(G):
-        g.tensor.wait_ge(S["q_w%s%d" % (tag, i)], 1)
-        g.tensor.matmul_mx(z[:, BANK * i:BANK * i + NC], w[0][:, NC * i:NC * i + NC], w[1][:, NC * i:NC * i + NC],
-                           x[0][:], x[1][:], True, True).then_inc(S["z_%s%d" % (tag, i)], 1)
-        g.scalar.wait_ge(S["z_%s%d" % (tag, i)], 1)
-        g.scalar.activation(tile[:, i:TW:4], z[:, BANK * i:BANK * i + NC], ActivationFunctionType.Relu,
-                            scale=C).then_inc(S["a_" + tag], 1)
-
-
-def _pack_inputs(g, T, S, xt, wt, x, w, tag):
+def _path(g, S, tag, xt, wt, x, w, z, tile, pieces, last_on_vector):
     g.vector.wait_ge(S["ld_x" + tag], 16)
     g.vector.quantize_mx(x[0][:], x[1][:], xt[:]).then_inc(S["q_x" + tag], 1)
-    g.vector.wait_ge(S["ld_w" + tag], 16)
-    for i in range(G):
-        g.vector.quantize_mx(w[0][:, NC * i:NC * i + NC], w[1][:, NC * i:NC * i + NC],
-                             wt[:, TW * i:TW * i + TW]).then_inc(S["q_w%s%d" % (tag, i)], 1)
+    g.tensor.wait_ge(S["q_x" + tag], 1)
+    n_scalar = 0
+    for p, (a, b) in enumerate(pieces):
+        g.vector.wait_ge(S["ld_w%s%d" % (tag, p)], 16)
+        for i in range(a, b):
+            g.vector.quantize_mx(w[0][:, NC * i:NC * i + NC], w[1][:, NC * i:NC * i + NC],
+                                 wt[:, TW * i:TW * i + TW]).then_inc(S["q_w%s%d" % (tag, i)], 1)
+            g.tensor.wait_ge(S["q_w%s%d" % (tag, i)], 1)
+            bank = z[:, BANK * i:BANK * i + NC]
+            g.tensor.matmul_mx(bank, w[0][:, NC * i:NC * i + NC], w[1][:, NC * i:NC * i + NC],
+                               x[0][:], x[1][:], True, True).then_inc(S["z_%s%d" % (tag, i)], 1)
+            if last_on_vector and i == G - 1:
+                g.vector.wait_ge(S["z_%s%d" % (tag, i)], 1)
+                g.vector.tensor_scalar(tile[:, i:TW:4], bank, 0.0, C, AluOpType.max,
+                                       AluOpType.mult).then_inc(S["v_" + tag], 1)
+                g.vector.wait_ge(S["v_" + tag], 1)
+            else:
+                g.scalar.wait_ge(S["z_%s%d" % (tag, i)], 1)
+                g.scalar.activation(tile[:, i:TW:4], bank, ActivationFunctionType.Relu,
+                                    scale=C).then_inc(S["a_" + tag], 1)
+                n_scalar += 1
+    g.vector.wait_ge(S["a_" + tag], n_scalar)
+    return n_scalar
 
 
 def rank_program(g, core, T, topo):
@@ -87,71 +78,80 @@ def rank_program(g, core, T, topo):
         return
     S = T.sem
     cores = list(T.cores)
-    far, near = _lanes(topo, cores, core)
-    for c, _m in far + near:
+    near, twin, cross = _kin(topo, cores, core)
+    for c in (near, twin, cross):
         if not topo.may_write(core, c):
             raise ValueError("no direct write from core %d to core %d" % (core, c))
+    out = topo.mask(core, twin) & topo.mask(core, cross)
+    home = topo.mask(core, near)
+    stay = home & ~out
+    n_out, n_home, n_stay = _count(out), _count(home), _count(stay)
 
     def slot(j):
         return slice(NC * j, NC * j + NC)
 
-    g.sync.dma_start(T.xk_t[:], T.xk[:]).then_inc(S.ld_xk, 16)
-    g.scalar.dma_start(T.wk_t[:], T.wk[:]).then_inc(S.ld_wk, 16)
-    g.sync.dma_start(T.xq_t[:], T.xq[:]).then_inc(S.ld_xq, 16)
-    g.scalar.dma_start(T.wq_t[:], T.wq[:]).then_inc(S.ld_wq, 16)
+    def to(c):
+        return DstId(rid=topo.addr(c)[0], pnc=topo.addr(c)[1])
 
-    _pack_inputs(g, T, S, T.xk_t, T.wk_t, (T.xk_c, T.xk_s), (T.wk_c, T.wk_s), "k")
-    _project(g, T, S, (T.xk_c, T.xk_s), (T.wk_c, T.wk_s), T.zk, T.k_t, "k")
-    g.vector.wait_ge(S.a_k, G)
+    def cols(p):
+        return slice(TW * p[0], TW * p[1])
+
+    g.sync.dma_start(T.xk_t[:], T.xk[:]).then_inc(S.ld_xk, 16)
+    g.scalar.dma_start(T.wk_t[:, cols(WK_PIECES[0])], T.wk[:, cols(WK_PIECES[0])]).then_inc(S.ld_wk0, 16)
+    g.sync.dma_start(T.wk_t[:, cols(WK_PIECES[1])], T.wk[:, cols(WK_PIECES[1])]).then_inc(S.ld_wk1, 16)
+    g.scalar.dma_start(T.wk_t[:, cols(WK_PIECES[2])], T.wk[:, cols(WK_PIECES[2])]).then_inc(S.ld_wk2, 16)
+    g.sync.dma_start(T.xq_t[:], T.xq[:]).then_inc(S.ld_xq, 16)
+    g.scalar.dma_start(T.wq_t[:, cols(WQ_PIECES[0])], T.wq[:, cols(WQ_PIECES[0])]).then_inc(S.ld_wq0, 16)
+    g.sync.dma_start(T.wq_t[:, cols(WQ_PIECES[1])], T.wq[:, cols(WQ_PIECES[1])]).then_inc(S.ld_wq1, 16)
+
+    n_ak = _path(g, S, "k", T.xk_t, T.wk_t, (T.xk_c, T.xk_s), (T.wk_c, T.wk_s), T.zk, T.k_t, WK_PIECES, True)
     g.vector.quantize_mx(T.ka_c[:, slot(r)], T.ka_s[:, slot(r)], T.k_t[:]).then_inc(S.kq, 1)
 
     codes = T.ka_c[:, slot(r)].bitcast(dt.uint8)
     plane = T.ka_s[:, slot(r)]
+    jx = cores.index(cross)
     g.wait_ge(S.kq, 1)
-    for ap in (codes, plane):
-        g.remote_dma_fused([RemoteDMATransfer(dst_ids=[DstId(rid=topo.addr(c)[0], pnc=topo.addr(c)[1])],
-                                              dma_engine_mask=m, remote_sem=S["arr%d" % r], src=ap, dst=ap)
-                            for c, m in far], local_sem=S.sent_far)
-    for ap in (codes, plane):
-        g.remote_dma_fused([RemoteDMATransfer(dst_ids=[DstId(rid=topo.addr(c)[0], pnc=topo.addr(c)[1])],
-                                              dma_engine_mask=m, remote_sem=S["arr%d" % r], src=ap, dst=ap)
-                            for c, m in near], local_sem=S.sent_near)
+    g.remote_dma_fused([RemoteDMATransfer(dst_ids=[to(cross)], dma_engine_mask=out, remote_sem=S["pl%d" % r],
+                                          src=plane, dst=plane)], local_sem=S.sent_p)
+    g.remote_dma_fused([RemoteDMATransfer(dst_ids=[to(cross), to(twin)], dma_engine_mask=out, remote_sem=S["cd%d" % r],
+                                          srcs=[codes], dsts=[codes, codes])], local_sem=S.sent)
+    g.remote_dma_fused([RemoteDMATransfer(dst_ids=[to(near)], dma_engine_mask=stay, remote_sem=S["cd%d" % r],
+                                          src=codes, dst=codes)], local_sem=S.sent)
+    g.remote_dma_fused([RemoteDMATransfer(dst_ids=[to(near)], dma_engine_mask=stay, remote_sem=S["pl%d" % r],
+                                          src=plane, dst=plane)], local_sem=S.sent)
+    g.wait_ge(S["pl%d" % jx], n_out)
+    xp = T.ka_s[:, slot(jx)]
+    g.remote_dma_fused([RemoteDMATransfer(dst_ids=[to(near)], dma_engine_mask=home, remote_sem=S["pl%d" % jx],
+                                          src=xp, dst=xp)], local_sem=S.sent)
 
-    _pack_inputs(g, T, S, T.xq_t, T.wq_t, (T.xq_c, T.xq_s), (T.wq_c, T.wq_s), "q")
-    _project(g, T, S, (T.xq_c, T.xq_s), (T.wq_c, T.wq_s), T.zq, T.q_t, "q")
-    g.vector.wait_ge(S.a_q, G)
+    _path(g, S, "q", T.xq_t, T.wq_t, (T.xq_c, T.xq_s), (T.wq_c, T.wq_s), T.zq, T.q_t, WQ_PIECES, False)
     g.vector.quantize_mx(T.q_c[:], T.q_s[:], T.q_t[:]).then_inc(S.qq, 1)
 
-    def landed(j):
-        f, n = _lanes(topo, cores, cores[j])
-        return 2 * len(_bits(dict(f + n)[core]))
-
-    order = ([r] + [cores.index(c) for c, _m in near]
-             + sorted([cores.index(c) for c, _m in far], key=lambda j: topo.die(cores[j]) != topo.die(core)))
+    order = [(r, 0, 0), (jx, n_out, n_out), (cores.index(near), n_stay, n_stay), (cores.index(twin), n_out, n_home)]
     g.tensor.wait_ge(S.qq, 1)
     g.tensor.wait_ge(S.kq, 1)
-    g.tensor.wait_ge(S.a_k, G)
-    g.sync.wait_ge(S.sent_far, 2 * sum(len(_bits(m)) for _c, m in far))
+    g.tensor.wait_ge(S.a_k, n_ak)
+    g.tensor.wait_ge(S.v_k, 1)
+    g.sync.wait_ge(S.sent_p, n_out)
     n_a = 0
-    for n, j in enumerate(order):
+    for n, (j, n_cd, n_pl) in enumerate(order):
         if j != r:
-            g.tensor.wait_ge(S["arr%d" % j], landed(j))
+            g.tensor.wait_ge(S["cd%d" % j], n_cd)
+            g.tensor.wait_ge(S["pl%d" % j], n_pl)
         bank = T.zk[:, BANK * j:BANK * j + NC]
         g.tensor.matmul_mx(bank, T.ka_c[:, slot(j)], T.ka_s[:, slot(j)], T.q_c[:], T.q_s[:],
                            True, True).then_inc(S["y%d" % j], 1)
-        if n % 2 == 0:
-            g.vector.wait_ge(S["y%d" % j], 1)
-            g.vector.tensor_copy(T.y_t[:, slot(j)], bank).then_inc(S["c%d" % j], 1)
-        else:
+        if n == len(order) - 1:
             g.scalar.wait_ge(S["y%d" % j], 1)
             g.scalar.activation(T.y_t[:, slot(j)], bank, ActivationFunctionType.Copy).then_inc(S["c%d" % j], 1)
-        if n == len(order) - 1:
             g.scalar.wait_ge(S["c%d" % j], 1)
             g.scalar.dma_start(T.y[:, slot(j)], T.y_t[:, slot(j)]).then_inc(S.st_b, 16)
         else:
+            g.vector.wait_ge(S["y%d" % j], 1)
+            g.vector.tensor_copy(T.y_t[:, slot(j)], bank).then_inc(S["c%d" % j], 1)
             g.sync.wait_ge(S["c%d" % j], 1)
             g.sync.dma_start(T.y[:, slot(j)], T.y_t[:, slot(j)]).then_inc(S.st_a, 16)
             n_a += 16
-    g.wait_ge(S.sent_near, 2 * sum(len(_bits(m)) for _c, m in near))
+    g.wait_ge(S.sent, n_out + 2 * n_stay + n_home)
     g.sync.wait_ge(S.st_a, n_a)
     g.scalar.wait_ge(S.st_b, 16)

from concourse.bass import DstId, RemoteDMATransfer
from concourse.mybir import dt, ActivationFunctionType, AluOpType

N, NC, G = 4, 128, 4
TW = 4 * NC
BANK = 512
C = 0.019
WK_PIECES = ((0, 2), (2, 3), (3, 4))
WQ_PIECES = ((0, 2), (2, 4))

SCRATCH = {
    "xk_t": ("sbuf", [128, TW], "bfloat16"), "wk_t": ("sbuf", [128, G * TW], "bfloat16"),
    "xq_t": ("sbuf", [128, TW], "bfloat16"), "wq_t": ("sbuf", [128, G * TW], "bfloat16"),
    "xk_c": ("sbuf", [128, NC], "float8_e4m3fn_x4"), "xk_s": ("sbuf", [128, NC], "uint8"),
    "wk_c": ("sbuf", [128, G * NC], "float8_e4m3fn_x4"), "wk_s": ("sbuf", [128, G * NC], "uint8"),
    "xq_c": ("sbuf", [128, NC], "float8_e4m3fn_x4"), "xq_s": ("sbuf", [128, NC], "uint8"),
    "wq_c": ("sbuf", [128, G * NC], "float8_e4m3fn_x4"), "wq_s": ("sbuf", [128, G * NC], "uint8"),
    "k_t": ("sbuf", [128, TW], "bfloat16"), "q_t": ("sbuf", [128, TW], "bfloat16"),
    "q_c": ("sbuf", [128, NC], "float8_e4m3fn_x4"), "q_s": ("sbuf", [128, NC], "uint8"),
    "ka_c": ("sbuf", [128, N * NC], "float8_e4m3fn_x4"), "ka_s": ("sbuf", [128, N * NC], "uint8"),
    "zk": ("psum", [128, G * BANK], "float32"), "zq": ("psum", [128, G * BANK], "float32"),
    "y_t": ("sbuf", [128, N * NC], "float32"),
}
SEMAPHORES = (["ld_xk", "ld_xq", "q_xk", "q_xq", "a_k", "a_q", "v_k", "v_q", "kq", "qq", "sent", "sent_p",
               "st_a", "st_b"]
              + ["ld_wk%d" % i for i in range(len(WK_PIECES))] + ["ld_wq%d" % i for i in range(len(WQ_PIECES))]
              + ["q_wk%d" % i for i in range(G)] + ["q_wq%d" % i for i in range(G)]
              + ["z_k%d" % i for i in range(G)] + ["z_q%d" % i for i in range(G)]
              + ["cd%d" % j for j in range(N)] + ["pl%d" % j for j in range(N)]
              + ["y%d" % j for j in range(N)] + ["c%d" % j for j in range(N)])


def _count(mask):
    return sum((mask >> b) & 1 for b in range(mask.bit_length()))


def _kin(topo, cores, me):
    near = [c for c in cores if c != me and topo.chip(c) == topo.chip(me)]
    far = [c for c in cores if topo.chip(c) != topo.chip(me)]
    twin = [c for c in far if topo.die(c) == topo.die(me)]
    cross = [c for c in far if topo.die(c) != topo.die(me)]
    if len(near) != 1 or len(twin) != 1 or len(cross) != 1:
        raise ValueError("the plan wants two ranks a chip, one a die")
    return near[0], twin[0], cross[0]


def _path(g, S, tag, xt, wt, x, w, z, tile, pieces, last_on_vector):
    g.vector.wait_ge(S["ld_x" + tag], 16)
    g.vector.quantize_mx(x[0][:], x[1][:], xt[:]).then_inc(S["q_x" + tag], 1)
    g.tensor.wait_ge(S["q_x" + tag], 1)
    n_scalar = 0
    for p, (a, b) in enumerate(pieces):
        g.vector.wait_ge(S["ld_w%s%d" % (tag, p)], 16)
        for i in range(a, b):
            g.vector.quantize_mx(w[0][:, NC * i:NC * i + NC], w[1][:, NC * i:NC * i + NC],
                                 wt[:, TW * i:TW * i + TW]).then_inc(S["q_w%s%d" % (tag, i)], 1)
            g.tensor.wait_ge(S["q_w%s%d" % (tag, i)], 1)
            bank = z[:, BANK * i:BANK * i + NC]
            g.tensor.matmul_mx(bank, w[0][:, NC * i:NC * i + NC], w[1][:, NC * i:NC * i + NC],
                               x[0][:], x[1][:], True, True).then_inc(S["z_%s%d" % (tag, i)], 1)
            if last_on_vector and i == G - 1:
                g.vector.wait_ge(S["z_%s%d" % (tag, i)], 1)
                g.vector.tensor_scalar(tile[:, i:TW:4], bank, 0.0, C, AluOpType.max,
                                       AluOpType.mult).then_inc(S["v_" + tag], 1)
                g.vector.wait_ge(S["v_" + tag], 1)
            else:
                g.scalar.wait_ge(S["z_%s%d" % (tag, i)], 1)
                g.scalar.activation(tile[:, i:TW:4], bank, ActivationFunctionType.Relu,
                                    scale=C).then_inc(S["a_" + tag], 1)
                n_scalar += 1
    g.vector.wait_ge(S["a_" + tag], n_scalar)
    return n_scalar


def rank_program(g, core, T, topo):
    r = T.rank_of(core)
    if r is None:
        return
    S = T.sem
    cores = list(T.cores)
    near, twin, cross = _kin(topo, cores, core)
    for c in (near, twin, cross):
        if not topo.may_write(core, c):
            raise ValueError("no direct write from core %d to core %d" % (core, c))
    out = topo.mask(core, twin) & topo.mask(core, cross)
    home = topo.mask(core, near)
    stay = home & ~out
    n_out, n_home, n_stay = _count(out), _count(home), _count(stay)

    def slot(j):
        return slice(NC * j, NC * j + NC)

    def to(c):
        return DstId(rid=topo.addr(c)[0], pnc=topo.addr(c)[1])

    def cols(p):
        return slice(TW * p[0], TW * p[1])

    g.sync.dma_start(T.xk_t[:], T.xk[:]).then_inc(S.ld_xk, 16)
    g.scalar.dma_start(T.wk_t[:, cols(WK_PIECES[0])], T.wk[:, cols(WK_PIECES[0])]).then_inc(S.ld_wk0, 16)
    g.sync.dma_start(T.wk_t[:, cols(WK_PIECES[1])], T.wk[:, cols(WK_PIECES[1])]).then_inc(S.ld_wk1, 16)
    g.scalar.dma_start(T.wk_t[:, cols(WK_PIECES[2])], T.wk[:, cols(WK_PIECES[2])]).then_inc(S.ld_wk2, 16)
    g.sync.dma_start(T.xq_t[:], T.xq[:]).then_inc(S.ld_xq, 16)
    g.scalar.dma_start(T.wq_t[:, cols(WQ_PIECES[0])], T.wq[:, cols(WQ_PIECES[0])]).then_inc(S.ld_wq0, 16)
    g.sync.dma_start(T.wq_t[:, cols(WQ_PIECES[1])], T.wq[:, cols(WQ_PIECES[1])]).then_inc(S.ld_wq1, 16)

    n_ak = _path(g, S, "k", T.xk_t, T.wk_t, (T.xk_c, T.xk_s), (T.wk_c, T.wk_s), T.zk, T.k_t, WK_PIECES, True)
    g.vector.quantize_mx(T.ka_c[:, slot(r)], T.ka_s[:, slot(r)], T.k_t[:]).then_inc(S.kq, 1)

    codes = T.ka_c[:, slot(r)].bitcast(dt.uint8)
    plane = T.ka_s[:, slot(r)]
    jx = cores.index(cross)
    g.wait_ge(S.kq, 1)
    g.remote_dma_fused([RemoteDMATransfer(dst_ids=[to(cross)], dma_engine_mask=out, remote_sem=S["pl%d" % r],
                                          src=plane, dst=plane)], local_sem=S.sent_p)
    g.remote_dma_fused([RemoteDMATransfer(dst_ids=[to(cross), to(twin)], dma_engine_mask=out, remote_sem=S["cd%d" % r],
                                          srcs=[codes], dsts=[codes, codes])], local_sem=S.sent)
    g.remote_dma_fused([RemoteDMATransfer(dst_ids=[to(near)], dma_engine_mask=stay, remote_sem=S["cd%d" % r],
                                          src=codes, dst=codes)], local_sem=S.sent)
    g.remote_dma_fused([RemoteDMATransfer(dst_ids=[to(near)], dma_engine_mask=stay, remote_sem=S["pl%d" % r],
                                          src=plane, dst=plane)], local_sem=S.sent)
    g.wait_ge(S["pl%d" % jx], n_out)
    xp = T.ka_s[:, slot(jx)]
    g.remote_dma_fused([RemoteDMATransfer(dst_ids=[to(near)], dma_engine_mask=home, remote_sem=S["pl%d" % jx],
                                          src=xp, dst=xp)], local_sem=S.sent)

    _path(g, S, "q", T.xq_t, T.wq_t, (T.xq_c, T.xq_s), (T.wq_c, T.wq_s), T.zq, T.q_t, WQ_PIECES, False)
    g.vector.quantize_mx(T.q_c[:], T.q_s[:], T.q_t[:]).then_inc(S.qq, 1)

    order = [(r, 0, 0), (jx, n_out, n_out), (cores.index(near), n_stay, n_stay), (cores.index(twin), n_out, n_home)]
    g.tensor.wait_ge(S.qq, 1)
    g.tensor.wait_ge(S.kq, 1)
    g.tensor.wait_ge(S.a_k, n_ak)
    g.tensor.wait_ge(S.v_k, 1)
    g.sync.wait_ge(S.sent_p, n_out)
    n_a = 0
    for n, (j, n_cd, n_pl) in enumerate(order):
        if j != r:
            g.tensor.wait_ge(S["cd%d" % j], n_cd)
            g.tensor.wait_ge(S["pl%d" % j], n_pl)
        bank = T.zk[:, BANK * j:BANK * j + NC]
        g.tensor.matmul_mx(bank, T.ka_c[:, slot(j)], T.ka_s[:, slot(j)], T.q_c[:], T.q_s[:],
                           True, True).then_inc(S["y%d" % j], 1)
        if n == len(order) - 1:
            g.scalar.wait_ge(S["y%d" % j], 1)
            g.scalar.activation(T.y_t[:, slot(j)], bank, ActivationFunctionType.Copy).then_inc(S["c%d" % j], 1)
            g.scalar.wait_ge(S["c%d" % j], 1)
            g.scalar.dma_start(T.y[:, slot(j)], T.y_t[:, slot(j)]).then_inc(S.st_b, 16)
        else:
            g.vector.wait_ge(S["y%d" % j], 1)
            g.vector.tensor_copy(T.y_t[:, slot(j)], bank).then_inc(S["c%d" % j], 1)
            g.sync.wait_ge(S["c%d" % j], 1)
            g.sync.dma_start(T.y[:, slot(j)], T.y_t[:, slot(j)]).then_inc(S.st_a, 16)
            n_a += 16
    g.wait_ge(S.sent, n_out + 2 * n_stay + n_home)
    g.sync.wait_ge(S.st_a, n_a)
    g.scalar.wait_ge(S.st_b, 16)
